import numpy as np
import ml_dtypes


def mxq(x, axis, fmt="e4m3"):
    dtype, down = {"e4m3": (ml_dtypes.float8_e4m3fn, 7), "e5m2": (ml_dtypes.float8_e5m2, 14)}[fmt]
    v = np.moveaxis(np.asarray(x, np.float32).astype(ml_dtypes.bfloat16).astype(np.float64), axis, -1)
    blocks = v.reshape(v.shape[:-1] + (-1, 32))
    amax = np.abs(blocks).max(-1, keepdims=True)
    byte = np.maximum(np.where(amax > 0, np.frexp(amax)[1] - 1 + 127, 0) - down, 1)
    scale = np.exp2(byte - 127.0)
    codes = (blocks / scale).astype(np.float32).astype(dtype).astype(np.float64)
    return np.moveaxis((codes * scale).reshape(v.shape), -1, axis)


WIDE = False


def mx_kscale(k):
    if not WIDE:
        return np.ones(k)
    levels = np.array([10, -10, 5, -5, 0])
    if k % 512:
        return np.exp2(np.random.permutation(np.resize(levels, k // 32))).repeat(32)
    a = np.empty((k // 512, 16))
    for p in range(k // 512):
        a[p, :8] = np.random.permutation(np.resize(levels, 8))
        for g in range(8):
            far = levels[np.abs(levels - a[p, g]) >= 10]
            a[p, g + 8] = far[np.random.randint(len(far))]
    return np.exp2(a.ravel()).repeat(32)


def f64(x):
    return np.asarray(x).astype(np.float64)


def striped(idx):
    return np.tile(idx.reshape(-1, 16).T, (8, 1)).astype(np.uint16)


def unstriped(offs):
    return offs[:16].T.reshape(-1).astype(np.int64)


K, T, S, D, H, N = 1024, 1024, 512, 3, 512, 128


def setup_inputs():
    n = np.random.standard_normal
    s = mx_kscale(K)[:, None]
    u = mx_kscale(H)
    return {
        "xT": (n((K, T)) * s).astype(np.float32),
        "w1": (n((K, H)) / np.sqrt(K) / s * u).astype(np.float32),
        "w2": (n((H, N)) / np.sqrt(H) / u[:, None]).astype(np.float32),
        "taps": (n((H, D)) / np.sqrt(D)).astype(np.float32),
        "offs": striped(np.random.permutation(T)[:S]),
    }


def reference(xT, w1, w2, taps, offs):
    xq = mxq(f64(xT)[:, unstriped(offs)], 0, "e4m3")
    h = mxq(f64(w1), 0, "e4m3").T @ xq
    z = f64(taps)[:, 0:1] * h + f64(taps)[:, 1:2] * (np.pad(h, ((0, 0), (1, 0)))[:, :S]) + f64(taps)[:, 2:3] * (np.pad(h, ((0, 0), (2, 0)))[:, :S])
    return mxq(f64(w2), 0, "e4m3").T @ mxq(z, 0, "e4m3")

@@ -1,0 +1,209 @@
+from contextlib import ExitStack
+
+import concourse.mybir as mybir
+
+K, T, S, D, H, N = 1024, 1024, 512, 3, 512, 128
+FLOPS = 2 * K * H * S + 2 * H * N * S
+
+F32 = mybir.dt.float32
+BF16 = mybir.dt.bfloat16
+U32 = mybir.dt.uint32
+U16 = mybir.dt.uint16
+U8 = mybir.dt.uint8
+FP8X4 = mybir.dt.float8_e4m3fn_x4
+MULT = mybir.AluOpType.mult
+ADD = mybir.AluOpType.add
+COPY = mybir.ActivationFunctionType.Copy
+
+P = 128
+PACK = 4
+K_PASS = P * PACK
+PASSES = K // K_PASS
+PAD = 4
+X_VECTOR_COLS = (640, 640, 384, 320)
+SPARE = 8
+W1_ON_VECTOR = ((), (0, 1))
+RANGES = ((0, 256), (256, 384), (384, 512))
+
+
+def tile_picked_dconv_none_e_kernel(tc, xT, w1, w2, taps, offs, out):
+    nc = tc.nc
+    with ExitStack() as ctx:
+        keep = ctx.enter_context(tc.tile_pool(name="keep", bufs=1))
+        psum = ctx.enter_context(tc.psum_pool(name="psum", bufs=1))
+
+        offsets = keep.tile([P, S // 16], U16, name="offsets")
+        tap = [keep.tile([P, D], F32, name=f"tap{t}") for t in range(PACK)]
+        x_raw = [keep.tile([P, 2, T], F32, name=f"x_raw{i}") for i in range(2 * PASSES)]
+        w1_raw = [keep.tile([P, PACK, H], F32, name=f"w1_raw{g}") for g in range(PASSES)]
+        w2_raw = keep.tile([P, PACK, N], F32, name="w2_raw")
+
+        x_rows = xT.rearrange("(g p u e) t -> g u p e t", g=PASSES, p=P, u=2, e=2)
+        w1_rows = w1.rearrange("(g p j) h -> g p j h", g=PASSES, j=PACK)
+        nc.sync.dma_start(out=x_raw[0][:], in_=x_rows[0, 0])
+        nc.sync.dma_start(offsets[:], offs)
+        tap_rows = taps.rearrange("(b t r) d -> t b r d", t=PACK, r=8)
+        for t in range(PACK):
+            nc.gpsimd.dma_start(out=tap[t][:], in_=tap_rows[t])
+        for i in range(1, 2 * PASSES):
+            nc.sync.dma_start(out=x_raw[i][:], in_=x_rows[i // 2, i % 2])
+        for g in range(PASSES):
+            nc.sync.dma_start(out=w1_raw[g][:], in_=w1_rows[g])
+        w2_rows = w2.rearrange("(b t r) n -> t b r n", t=PACK, r=8)
+        for t in range(PACK):
+            nc.sync.dma_start(out=w2_raw[:, t, :], in_=w2_rows[t])
+
+        late = keep.tile([P, PACK, PAD + S], F32, name="late")
+        mid = keep.tile([P, PACK, PAD + S], F32, name="mid")
+        nc.vector.memset(mid[:, :, 0:PAD], 0.0)
+        nc.scalar.activation(out=late[:, :, 0:PAD], in_=mid[:, :, 0:PAD], func=COPY)
+
+        pairs = keep.tile([P, 2 * PASSES * T * 2], BF16, name="pairs", align_bytes=64)
+        pair_words = pairs[:].bitcast(U32)
+        for i in range(1, 2 * PASSES):
+            nc.vector.memset(pairs[:, 2 * T * i : 2 * (T * i + SPARE)], 0.0)
+        picked = [keep.tile([P, S * PACK], BF16, name=f"picked{g}", align_bytes=64) for g in range(PASSES)]
+        h = [psum.tile([P, S], F32, name=f"h{t}") for t in range(PACK)]
+        x_q = {}
+        w1_bf = {}
+
+        def pick(g, u):
+            i = 2 * g + u
+            pairs_v = pairs[:, 2 * T * i : 2 * T * (i + 1)].rearrange("p (t e) -> p t e", e=2)
+            window = pair_words[:, T * i : min(T * (i + 1) + SPARE, 2 * PASSES * T)]
+            src = x_raw[i][:].rearrange("p e t -> p t e")
+            cut = X_VECTOR_COLS[i]
+            nc.scalar.copy(out=pairs_v[:, cut:, :], in_=src[:, cut:, :])
+            nc.vector.tensor_copy(out=pairs_v[:, :cut, :], in_=src[:, :cut, :])
+            picked_words = picked[g][:].bitcast(U32).rearrange("p (n u) -> p n u", u=2)
+            nc.vector.tensor_copy(out=picked_words[:, :, u], in_=window.indirect(offsets[:]))
+
+        def quantize_x(g, tag):
+            codes = keep.tile([P, S], U32, name=f"x_codes{g}", tag=tag, align_bytes=64)
+            scales = keep.tile([P, S], U8, name=f"x_scales{g}", align_bytes=64)
+            nc.vector.quantize_mx(out=codes[:].bitcast(FP8X4), scales=scales[:], in_=picked[g][:])
+            x_q[g] = (codes, scales)
+
+        def round_w1(g, t, tag, on_vector):
+            src = w1_raw[g][:].rearrange("p j (b t r) -> p t b r j", t=PACK, r=8)
+            bf = keep.tile([P, K_PASS], BF16, name=f"w1_bf{g}{t}", tag=tag, align_bytes=64)
+            dst = bf[:].rearrange("p (b r j) -> p b r j", r=8, j=PACK)
+            if on_vector:
+                nc.vector.tensor_copy(out=dst, in_=src[:, t])
+            else:
+                nc.scalar.copy(out=dst, in_=src[:, t])
+            w1_bf[g, t] = bf
+
+        def quantize_w1(g, t):
+            codes = keep.tile([P, P], U32, name=f"w1_codes{g}{t}", align_bytes=64)
+            scales = keep.tile([P, P], U8, name=f"w1_scales{g}{t}", align_bytes=64)
+            nc.vector.quantize_mx(out=codes[:].bitcast(FP8X4), scales=scales[:], in_=w1_bf[g, t][:])
+            nc.tensor.matmul_mx(
+                out=h[t][:],
+                lhsT=codes[:].bitcast(FP8X4),
+                lhsT_scale=scales[:],
+                rhs=x_q[g][0][:].bitcast(FP8X4),
+                rhs_scale=x_q[g][1][:],
+                start=(g == 0),
+                stop=(g == PASSES - 1),
+            )
+
+        def late_term(t):
+            nc.scalar.activation(out=late[:, t, PAD:], in_=h[t][:], func=COPY, scale=tap[t][:, 2:3])
+
+        pick(0, 0)
+        pick(0, 1)
+        quantize_x(0, "x_codes0")
+        pick(1, 0)
+        pick(1, 1)
+        for t in range(PACK):
+            round_w1(0, t, "abcd"[t], False)
+        quantize_w1(0, 0)
+        quantize_x(1, "a")
+        quantize_w1(0, 1)
+        quantize_w1(0, 2)
+        round_w1(1, 0, "c", True)
+        round_w1(1, 2, "b", False)
+        round_w1(1, 3, "e", False)
+        quantize_w1(1, 0)
+        late_term(0)
+        quantize_w1(0, 3)
+        round_w1(1, 1, "d", True)
+        for t in range(1, PACK):
+            quantize_w1(1, t)
+            late_term(t)
+        w2_bf = keep.tile([P, N * PACK], BF16, name="w2_bf", tag="e", align_bytes=64)
+        nc.scalar.copy(out=w2_bf[:].rearrange("p (n j) -> p n j", j=PACK), in_=w2_raw[:].rearrange("p j n -> p n j"))
+        w2_codes = keep.tile([P, N], U32, name="w2_codes", align_bytes=64)
+        w2_scales = keep.tile([P, N], U8, name="w2_scales", align_bytes=64)
+        nc.vector.quantize_mx(out=w2_codes[:].bitcast(FP8X4), scales=w2_scales[:], in_=w2_bf[:])
+
+        z_tiles = []
+        for r, (a, b) in enumerate(RANGES):
+            z = keep.tile([P, PACK, b - a], BF16, name=f"z{r}", align_bytes=64)
+            z_tiles.append(z)
+
+        def first_sum(t):
+            a, b = 0, S
+            nc.vector.scalar_tensor_tensor(
+                out=mid[:, t, PAD + a : PAD + b],
+                in0=h[t][:, a:b],
+                scalar=tap[t][:, 1:2],
+                in1=late[:, t, PAD + a - 1 : PAD + b - 1],
+                op0=MULT,
+                op1=ADD,
+            )
+
+        def second_sum(r, t):
+            a, b = RANGES[r]
+            nc.vector.scalar_tensor_tensor(
+                out=z_tiles[r][:, t, :],
+                in0=h[t][:, a:b],
+                scalar=tap[t][:, 0:1],
+                in1=mid[:, t, PAD + a - 1 : PAD + b - 1],
+                op0=MULT,
+                op1=ADD,
+            )
+
+        def weave(r):
+            a, b = RANGES[r]
+            woven = keep.tile([P, (b - a) * PACK], BF16, name=f"woven{r}", align_bytes=64)
+            dst = woven[:].rearrange("p (n t) -> p n t", t=PACK)
+            src = z_tiles[r][:].rearrange("p t n -> p n t")
+            if r == len(RANGES) - 1:
+                nc.vector.tensor_copy(out=dst, in_=src)
+            else:
+                nc.scalar.copy(out=dst, in_=src)
+            return woven
+
+        def second_layer(r, woven):
+            a, b = RANGES[r]
+            codes = keep.tile([P, b - a], U32, name=f"z_codes{r}", align_bytes=64)
+            scales = keep.tile([P, b - a], U8, name=f"z_scales{r}", align_bytes=64)
+            nc.vector.quantize_mx(out=codes[:].bitcast(FP8X4), scales=scales[:], in_=woven[:])
+            acc = psum.tile([P, b - a], F32, name=f"acc{r}")
+            nc.tensor.matmul_mx(
+                out=acc[:],
+                lhsT=w2_codes[:].bitcast(FP8X4),
+                lhsT_scale=w2_scales[:],
+                rhs=codes[:].bitcast(FP8X4),
+                rhs_scale=scales[:],
+                start=True,
+                stop=True,
+            )
+            result = keep.tile([P, b - a], F32, name=f"result{r}")
+            nc.scalar.copy(out=result[:], in_=acc[:])
+            nc.sync.dma_start(out=out[:, a:b], in_=result[:])
+
+        first_sum(0)
+        for t in range(1, PACK):
+            first_sum(t)
+            second_sum(0, t - 1)
+        second_sum(0, PACK - 1)
+        waiting = weave(0)
+        for r in range(1, len(RANGES)):
+            for t in range(PACK):
+                second_sum(r, t)
+            second_layer(r - 1, waiting)
+            waiting = weave(r)
+        second_layer(len(RANGES) - 1, waiting)

@@ -8,6 +8,7 @@ FLOPS = 2 * K * H * S + 2 * H * N * S
 F32 = mybir.dt.float32
 BF16 = mybir.dt.bfloat16
 U32 = mybir.dt.uint32
+I32 = mybir.dt.int32
 U16 = mybir.dt.uint16
 U8 = mybir.dt.uint8
 FP8X4 = mybir.dt.float8_e4m3fn_x4
@@ -20,9 +21,7 @@ PACK = 4
 K_PASS = P * PACK
 PASSES = K // K_PASS
 PAD = 4
-X_VECTOR_COLS = (640, 640, 384, 320)
 SPARE = 8
-W1_ON_VECTOR = ((), (0, 1))
 RANGES = ((0, 256), (256, 384), (384, 512))
 
 
@@ -30,10 +29,12 @@ def tile_picked_dconv_none_e_kernel(tc, xT, w1, w2, taps, offs, out):
     nc = tc.nc
     with ExitStack() as ctx:
         keep = ctx.enter_context(tc.tile_pool(name="keep", bufs=1))
+        placed = ctx.enter_context(tc.tile_pool(name="placed", bufs=1))
         psum = ctx.enter_context(tc.psum_pool(name="psum", bufs=1))
 
         offsets = keep.tile([P, S // 16], U16, name="offsets")
-        tap = [keep.tile([P, D], F32, name=f"tap{t}") for t in range(PACK)]
+        tap_pair = [keep.tile([P, 2 * D], F32, name=f"tap{a}") for a in range(2)]
+        tap = [tap_pair[t // 2][:, (t % 2) * D : (t % 2 + 1) * D] for t in range(PACK)]
         x_raw = [keep.tile([P, 2, T], F32, name=f"x_raw{i}") for i in range(2 * PASSES)]
         w1_raw = [keep.tile([P, PACK, H], F32, name=f"w1_raw{g}") for g in range(PASSES)]
         w2_raw = keep.tile([P, PACK, N], F32, name="w2_raw")
@@ -42,62 +43,87 @@ def tile_picked_dconv_none_e_kernel(tc, xT, w1, w2, taps, offs, out):
         w1_rows = w1.rearrange("(g p j) h -> g p j h", g=PASSES, j=PACK)
         nc.sync.dma_start(out=x_raw[0][:], in_=x_rows[0, 0])
         nc.sync.dma_start(offsets[:], offs)
-        tap_rows = taps.rearrange("(b t r) d -> t b r d", t=PACK, r=8)
-        for t in range(PACK):
-            nc.gpsimd.dma_start(out=tap[t][:], in_=tap_rows[t])
+        tap_rows = taps.rearrange("(b a r e) d -> a b r (e d)", a=2, r=8, e=2)
+        for a in range(2):
+            nc.sync.dma_start(out=tap_pair[a][:], in_=tap_rows[a])
         for i in range(1, 2 * PASSES):
             nc.sync.dma_start(out=x_raw[i][:], in_=x_rows[i // 2, i % 2])
         for g in range(PASSES):
             nc.sync.dma_start(out=w1_raw[g][:], in_=w1_rows[g])
-        w2_rows = w2.rearrange("(b t r) n -> t b r n", t=PACK, r=8)
-        for t in range(PACK):
-            nc.sync.dma_start(out=w2_raw[:, t, :], in_=w2_rows[t])
+        w2_rows = w2.rearrange("(b a r e) n -> a b r (e n)", a=2, r=8, e=2)
+        for a in range(2):
+            nc.sync.dma_start(out=w2_raw[:, 2 * a : 2 * a + 2, :].rearrange("p e n -> p (e n)"), in_=w2_rows[a])
 
         late = keep.tile([P, PACK, PAD + S], F32, name="late")
         mid = keep.tile([P, PACK, PAD + S], F32, name="mid")
         nc.vector.memset(mid[:, :, 0:PAD], 0.0)
         nc.scalar.activation(out=late[:, :, 0:PAD], in_=mid[:, :, 0:PAD], func=COPY)
 
-        pairs = keep.tile([P, 2 * PASSES * T * 2], BF16, name="pairs", align_bytes=64)
-        pair_words = pairs[:].bitcast(U32)
-        for i in range(1, 2 * PASSES):
-            nc.vector.memset(pairs[:, 2 * T * i : 2 * (T * i + SPARE)], 0.0)
-        picked = [keep.tile([P, S * PACK], BF16, name=f"picked{g}", align_bytes=64) for g in range(PASSES)]
-        h = [psum.tile([P, S], F32, name=f"h{t}") for t in range(PACK)]
+        early = keep.tile([P, 2 * 2 * T], BF16, name="early", align_bytes=64)
+        third = keep.tile([P, 2 * T], BF16, name="third", align_bytes=64)
+        shared = keep.tile([P, T + S * PACK], BF16, name="shared", align_bytes=64)
+        picked1 = keep.tile([P, S * PACK], BF16, name="picked1", align_bytes=64)
+        nc.vector.memset(early[:, 2 * T : 2 * (T + SPARE)], 0.0)
+        pairs = [early[:, : 2 * T], early[:, 2 * T :], third[:], shared[:, : 2 * T]]
+        windows = [early[:, : 2 * (T + SPARE)]] + pairs[1:]
+        picked = [shared[:, T : T + S * PACK], picked1[:]]
         x_q = {}
-        w1_bf = {}
 
-        def pick(g, u):
-            i = 2 * g + u
-            pairs_v = pairs[:, 2 * T * i : 2 * T * (i + 1)].rearrange("p (t e) -> p t e", e=2)
-            window = pair_words[:, T * i : min(T * (i + 1) + SPARE, 2 * PASSES * T)]
-            src = x_raw[i][:].rearrange("p e t -> p t e")
-            cut = X_VECTOR_COLS[i]
-            nc.scalar.copy(out=pairs_v[:, cut:, :], in_=src[:, cut:, :])
-            nc.vector.tensor_copy(out=pairs_v[:, :cut, :], in_=src[:, :cut, :])
-            picked_words = picked[g][:].bitcast(U32).rearrange("p (n u) -> p n u", u=2)
-            nc.vector.tensor_copy(out=picked_words[:, :, u], in_=window.indirect(offsets[:]))
-
-        def quantize_x(g, tag):
-            codes = keep.tile([P, S], U32, name=f"x_codes{g}", tag=tag, align_bytes=64)
+        def x_tiles(g, offset):
+            if offset is None:
+                codes = keep.tile([P, S], U32, name=f"x_codes{g}", align_bytes=64)
+            else:
+                codes = placed.tile([P, S], U32, name=f"x_codes{g}", align_bytes=64, offset=offset)
             scales = keep.tile([P, S], U8, name=f"x_scales{g}", align_bytes=64)
-            nc.vector.quantize_mx(out=codes[:].bitcast(FP8X4), scales=scales[:], in_=picked[g][:])
             x_q[g] = (codes, scales)
 
-        def round_w1(g, t, tag, on_vector):
-            src = w1_raw[g][:].rearrange("p j (b t r) -> p t b r j", t=PACK, r=8)
-            bf = keep.tile([P, K_PASS], BF16, name=f"w1_bf{g}{t}", tag=tag, align_bytes=64)
-            dst = bf[:].rearrange("p (b r j) -> p b r j", r=8, j=PACK)
+        h = [psum.tile([P, S], F32, name=f"h{t}") for t in range(PACK)]
+        w1_bf = {}
+
+        def round_x(i, a, b, on_vector):
+            dst = pairs[i].rearrange("p (t e) -> p t e", e=2)[:, a:b, :]
+            src = x_raw[i][:].rearrange("p e t -> p t e")[:, a:b, :]
             if on_vector:
-                nc.vector.tensor_copy(out=dst, in_=src[:, t])
+                nc.vector.tensor_copy(out=dst, in_=src)
             else:
-                nc.scalar.copy(out=dst, in_=src[:, t])
+                nc.scalar.copy(out=dst, in_=src)
+
+        def pick(i, a, b):
+            g, u = divmod(i, 2)
+            nc.vector.tensor_copy(
+                out=picked[g].bitcast(U32).rearrange("p (n u) -> p n u", u=2)[:, a:b, u],
+                in_=windows[i].bitcast(U32).indirect(offsets[:, a // 16 : b // 16]),
+            )
+
+        def quantize_x(g, a, b):
+            codes, scales = x_q[g]
+            nc.vector.quantize_mx(
+                out=codes[:, a:b].bitcast(FP8X4), scales=scales[:, a:b], in_=picked[g][:, a * PACK : b * PACK]
+            )
+
+        def round_w1(g, t, bf, on_vector):
+            src = w1_raw[g][:].rearrange("p j (b a r e) -> p a e b r j", a=2, r=8, e=2)[:, t // 2, t % 2]
+            dst = bf.rearrange("p (b r j) -> p b r j", r=8, j=PACK)
+            if on_vector:
+                nc.vector.tensor_copy(out=dst, in_=src)
+            else:
+                nc.scalar.copy(out=dst, in_=src)
             w1_bf[g, t] = bf
 
-        def quantize_w1(g, t):
-            codes = keep.tile([P, P], U32, name=f"w1_codes{g}{t}", align_bytes=64)
+        def fresh(name, offset=None):
+            if offset is None:
+                tile = keep.tile([P, K_PASS], BF16, name=name, align_bytes=64)
+            else:
+                tile = placed.tile([P, K_PASS], BF16, name=name, align_bytes=64, offset=offset)
+            return tile[:]
+
+        def quantize_w1(g, t, offset=None):
+            if offset is None:
+                codes = keep.tile([P, P], U32, name=f"w1_codes{g}{t}", align_bytes=64)
+            else:
+                codes = placed.tile([P, P], U32, name=f"w1_codes{g}{t}", align_bytes=64, offset=offset)
             scales = keep.tile([P, P], U8, name=f"w1_scales{g}{t}", align_bytes=64)
-            nc.vector.quantize_mx(out=codes[:].bitcast(FP8X4), scales=scales[:], in_=w1_bf[g, t][:])
+            nc.vector.quantize_mx(out=codes[:].bitcast(FP8X4), scales=scales[:], in_=w1_bf[g, t])
             nc.tensor.matmul_mx(
                 out=h[t][:],
                 lhsT=codes[:].bitcast(FP8X4),
@@ -111,53 +137,64 @@ def tile_picked_dconv_none_e_kernel(tc, xT, w1, w2, taps, offs, out):
         def late_term(t):
             nc.scalar.activation(out=late[:, t, PAD:], in_=h[t][:], func=COPY, scale=tap[t][:, 2:3])
 
-        pick(0, 0)
-        pick(0, 1)
-        quantize_x(0, "x_codes0")
-        pick(1, 0)
-        pick(1, 1)
-        for t in range(PACK):
-            round_w1(0, t, "abcd"[t], False)
+        for i in range(2):
+            round_x(i, 640, T, False)
+            round_x(i, 0, 640, True)
+            pick(i, 0, S)
+        x_tiles(0, None)
+        quantize_x(0, 0, S)
+        round_x(2, 0, T, False)
+        round_x(3, 0, 576, False)
+        round_x(3, 576, T, True)
+        pick(2, 0, S)
+        pick(3, 0, S)
+        halves = ((0, S // 2), (S // 2, S))
+        round_w1(0, 0, fresh("w1_bf00", 2048), False)
+        for t in range(1, PACK):
+            round_w1(0, t, fresh(f"w1_bf0{t}"), False)
         quantize_w1(0, 0)
-        quantize_x(1, "a")
+        x_tiles(1, 2048)
+        quantize_x(1, 0, S)
         quantize_w1(0, 1)
         quantize_w1(0, 2)
-        round_w1(1, 0, "c", True)
-        round_w1(1, 2, "b", False)
-        round_w1(1, 3, "e", False)
-        quantize_w1(1, 0)
-        late_term(0)
-        quantize_w1(0, 3)
-        round_w1(1, 1, "d", True)
-        for t in range(1, PACK):
+        round_w1(1, 0, fresh("w1_bf10", 0), False)
+        round_w1(1, 1, fresh("w1_bf11"), True)
+        round_w1(1, 2, fresh("w1_bf12"), True)
+        round_w1(1, 3, fresh("w1_bf13"), False)
+        for t in range(PACK - 1):
             quantize_w1(1, t)
             late_term(t)
-        w2_bf = keep.tile([P, N * PACK], BF16, name="w2_bf", tag="e", align_bytes=64)
-        nc.scalar.copy(out=w2_bf[:].rearrange("p (n j) -> p n j", j=PACK), in_=w2_raw[:].rearrange("p j n -> p n j"))
+        quantize_w1(0, 3, 0)
+        quantize_w1(1, 3)
+        late_term(3)
+        w2_bf = keep.tile([P, N * PACK], BF16, name="w2_bf", align_bytes=64)
+        nc.scalar.copy(
+            out=w2_bf[:].rearrange("p (c i j) -> p c j i", i=4, j=PACK),
+            in_=w2_raw[:].rearrange("p j (c i) -> p c j i", i=4),
+        )
         w2_codes = keep.tile([P, N], U32, name="w2_codes", align_bytes=64)
         w2_scales = keep.tile([P, N], U8, name="w2_scales", align_bytes=64)
         nc.vector.quantize_mx(out=w2_codes[:].bitcast(FP8X4), scales=w2_scales[:], in_=w2_bf[:])
 
         z_tiles = []
-        for r, (a, b) in enumerate(RANGES):
-            z = keep.tile([P, PACK, b - a], BF16, name=f"z{r}", align_bytes=64)
+        for half in range(2):
+            z = keep.tile([P, PACK, S // 2], BF16, name=f"z{half}", align_bytes=64)
             z_tiles.append(z)
 
         def first_sum(t):
-            a, b = 0, S
             nc.vector.scalar_tensor_tensor(
-                out=mid[:, t, PAD + a : PAD + b],
-                in0=h[t][:, a:b],
+                out=mid[:, t, PAD:],
+                in0=h[t][:],
                 scalar=tap[t][:, 1:2],
-                in1=late[:, t, PAD + a - 1 : PAD + b - 1],
+                in1=late[:, t, PAD - 1 : PAD + S - 1],
                 op0=MULT,
                 op1=ADD,
             )
 
-        def second_sum(r, t):
-            a, b = RANGES[r]
+        def second_sum(half, t):
+            a, b = halves[half]
             nc.vector.scalar_tensor_tensor(
-                out=z_tiles[r][:, t, :],
+                out=z_tiles[half][:, t, :],
                 in0=h[t][:, a:b],
                 scalar=tap[t][:, 0:1],
                 in1=mid[:, t, PAD + a - 1 : PAD + b - 1],
@@ -167,9 +204,10 @@ def tile_picked_dconv_none_e_kernel(tc, xT, w1, w2, taps, offs, out):
 
         def weave(r):
             a, b = RANGES[r]
+            half, a0 = divmod(a, S // 2)
             woven = keep.tile([P, (b - a) * PACK], BF16, name=f"woven{r}", align_bytes=64)
-            dst = woven[:].rearrange("p (n t) -> p n t", t=PACK)
-            src = z_tiles[r][:].rearrange("p t n -> p n t")
+            dst = woven[:].rearrange("p (c i t) -> p c t i", i=4, t=PACK)
+            src = z_tiles[half][:, :, a0 : a0 + b - a].rearrange("p t (c i) -> p c t i", i=4)
             if r == len(RANGES) - 1:
                 nc.vector.tensor_copy(out=dst, in_=src)
             else:
@@ -199,11 +237,12 @@ def tile_picked_dconv_none_e_kernel(tc, xT, w1, w2, taps, offs, out):
         for t in range(1, PACK):
             first_sum(t)
             second_sum(0, t - 1)
+        second_sum(1, 0)
         second_sum(0, PACK - 1)
-        waiting = weave(0)
+        woven = [weave(0)]
+        for t in range(1, PACK):
+            second_sum(1, t)
+        second_layer(0, woven[0])
+        woven.extend(weave(r) for r in range(1, len(RANGES)))
         for r in range(1, len(RANGES)):
-            for t in range(PACK):
-                second_sum(r, t)
-            second_layer(r - 1, waiting)
-            waiting = weave(r)
-        second_layer(len(RANGES) - 1, waiting)
+            second_layer(r, woven[r])

@@ -43,13 +43,13 @@ def tile_picked_dconv_none_e_kernel(tc, xT, w1, w2, taps, offs, out):
         w1_rows = w1.rearrange("(g p j) h -> g p j h", g=PASSES, j=PACK)
         nc.sync.dma_start(out=x_raw[0][:], in_=x_rows[0, 0])
         nc.sync.dma_start(offsets[:], offs)
-        tap_rows = taps.rearrange("(b a r e) d -> a b r (e d)", a=2, r=8, e=2)
-        for a in range(2):
-            nc.sync.dma_start(out=tap_pair[a][:], in_=tap_rows[a])
         for i in range(1, 2 * PASSES):
             nc.sync.dma_start(out=x_raw[i][:], in_=x_rows[i // 2, i % 2])
         for g in range(PASSES):
             nc.sync.dma_start(out=w1_raw[g][:], in_=w1_rows[g])
+        tap_rows = taps.rearrange("(b a r e) d -> a b r (e d)", a=2, r=8, e=2)
+        for a in range(2):
+            nc.sync.dma_start(out=tap_pair[a][:], in_=tap_rows[a])
         w2_rows = w2.rearrange("(b a r e) n -> a b r (e n)", a=2, r=8, e=2)
         for a in range(2):
             nc.sync.dma_start(out=w2_raw[:, 2 * a : 2 * a + 2, :].rearrange("p e n -> p (e n)"), in_=w2_rows[a])
@@ -61,12 +61,13 @@ def tile_picked_dconv_none_e_kernel(tc, xT, w1, w2, taps, offs, out):
 
         early = keep.tile([P, 2 * 2 * T], BF16, name="early", align_bytes=64)
         third = keep.tile([P, 2 * T], BF16, name="third", align_bytes=64)
-        shared = keep.tile([P, T + S * PACK], BF16, name="shared", align_bytes=64)
+        fourth = keep.tile([P, 2 * T], BF16, name="fourth", align_bytes=64)
+        picked0 = keep.tile([P, S * PACK], BF16, name="picked0", align_bytes=64)
         picked1 = keep.tile([P, S * PACK], BF16, name="picked1", align_bytes=64)
         nc.vector.memset(early[:, 2 * T : 2 * (T + SPARE)], 0.0)
-        pairs = [early[:, : 2 * T], early[:, 2 * T :], third[:], shared[:, : 2 * T]]
+        pairs = [early[:, : 2 * T], early[:, 2 * T :], third[:], fourth[:]]
         windows = [early[:, : 2 * (T + SPARE)]] + pairs[1:]
-        picked = [shared[:, T : T + S * PACK], picked1[:]]
+        picked = [picked0[:], picked1[:]]
         x_q = {}
 
         def x_tiles(g, offset):
@@ -80,13 +81,15 @@ def tile_picked_dconv_none_e_kernel(tc, xT, w1, w2, taps, offs, out):
         h = [psum.tile([P, S], F32, name=f"h{t}") for t in range(PACK)]
         w1_bf = {}
 
-        def round_x(i, a, b, on_vector):
+        def round_x(i, a, b, engine):
             dst = pairs[i].rearrange("p (t e) -> p t e", e=2)[:, a:b, :]
             src = x_raw[i][:].rearrange("p e t -> p t e")[:, a:b, :]
-            if on_vector:
+            if engine == "vector":
                 nc.vector.tensor_copy(out=dst, in_=src)
-            else:
+            elif engine == "scalar":
                 nc.scalar.copy(out=dst, in_=src)
+            else:
+                nc.gpsimd.tensor_scalar(out=dst, in0=src, scalar1=1.0, scalar2=0.0, op0=MULT, op1=ADD)
 
         def pick(i, a, b):
             g, u = divmod(i, 2)
@@ -102,8 +105,8 @@ def tile_picked_dconv_none_e_kernel(tc, xT, w1, w2, taps, offs, out):
             )
 
         def round_w1(g, t, bf, on_vector):
-            src = w1_raw[g][:].rearrange("p j (b a r e) -> p a e b r j", a=2, r=8, e=2)[:, t // 2, t % 2]
-            dst = bf.rearrange("p (b r j) -> p b r j", r=8, j=PACK)
+            src = w1_raw[g][:].rearrange("p j (b a c i e) -> p a e b c j i", a=2, c=4, i=2, e=2)[:, t // 2, t % 2]
+            dst = bf.rearrange("p (b c i j) -> p b c j i", c=4, i=2, j=PACK)
             if on_vector:
                 nc.vector.tensor_copy(out=dst, in_=src)
             else:
@@ -138,14 +141,15 @@ def tile_picked_dconv_none_e_kernel(tc, xT, w1, w2, taps, offs, out):
             nc.scalar.activation(out=late[:, t, PAD:], in_=h[t][:], func=COPY, scale=tap[t][:, 2:3])
 
         for i in range(2):
-            round_x(i, 640, T, False)
-            round_x(i, 0, 640, True)
+            round_x(i, 640, T, "scalar")
+            round_x(i, 0, 640, "vector")
             pick(i, 0, S)
         x_tiles(0, None)
         quantize_x(0, 0, S)
-        round_x(2, 0, T, False)
-        round_x(3, 0, 576, False)
-        round_x(3, 576, T, True)
+        round_x(2, 0, 800, "scalar")
+        round_x(2, 800, T, "gpsimd")
+        round_x(3, 0, 608, "scalar")
+        round_x(3, 608, T, "gpsimd")
         pick(2, 0, S)
         pick(3, 0, S)
         halves = ((0, S // 2), (S // 2, S))

@@ -20,7 +20,7 @@ P = 128
 PACK = 4
 K_PASS = P * PACK
 PASSES = K // K_PASS
-PAD = 4
+PAD = 8
 SPARE = 8
 RANGES = ((0, 256), (256, 384), (384, 512))
 
@@ -171,6 +171,12 @@ def tile_picked_dconv_none_e_kernel(tc, xT, w1, w2, taps, offs, out):
         quantize_w1(0, 3, 0)
         quantize_w1(1, 3)
         late_term(3)
+        near = keep.tile([P, S], F32, name="near")
+        for a, b in halves:
+            nc.scalar.activation(out=near[:, a:b], in_=h[3][:, a:b], func=COPY, scale=tap[3][:, 1:2])
+            nc.gpsimd.tensor_tensor(
+                out=mid[:, 3, PAD + a : PAD + b], in0=near[:, a:b], in1=late[:, 3, PAD + a - 1 : PAD + b - 1], op=ADD
+            )
         w2_bf = keep.tile([P, N * PACK], BF16, name="w2_bf", align_bytes=64)
         nc.scalar.copy(
             out=w2_bf[:].rearrange("p (c i j) -> p c j i", i=4, j=PACK),
@@ -195,10 +201,10 @@ def tile_picked_dconv_none_e_kernel(tc, xT, w1, w2, taps, offs, out):
                 op1=ADD,
             )
 
-        def second_sum(half, t):
-            a, b = halves[half]
+        def second_sum(t, a, b):
+            half, a0 = divmod(a, S // 2)
             nc.vector.scalar_tensor_tensor(
-                out=z_tiles[half][:, t, :],
+                out=z_tiles[half][:, t, a0 : a0 + b - a],
                 in0=h[t][:, a:b],
                 scalar=tap[t][:, 0:1],
                 in1=mid[:, t, PAD + a - 1 : PAD + b - 1],
@@ -238,15 +244,20 @@ def tile_picked_dconv_none_e_kernel(tc, xT, w1, w2, taps, offs, out):
             nc.sync.dma_start(out=out[:, a:b], in_=result[:])
 
         first_sum(0)
-        for t in range(1, PACK):
-            first_sum(t)
-            second_sum(0, t - 1)
-        second_sum(1, 0)
-        second_sum(0, PACK - 1)
+        first_sum(1)
+        second_sum(0, *halves[0])
+        first_sum(2)
+        second_sum(1, *halves[0])
+        second_sum(0, *halves[1])
+        second_sum(2, *halves[0])
+        second_sum(3, *halves[0])
         woven = [weave(0)]
-        for t in range(1, PACK):
-            second_sum(1, t)
+        second_sum(1, *halves[1])
+        second_sum(2, *halves[1])
+        second_sum(3, *RANGES[1])
+        woven.append(weave(1))
+        second_sum(3, *RANGES[2])
         second_layer(0, woven[0])
-        woven.extend(weave(r) for r in range(1, len(RANGES)))
+        woven.append(weave(2))
         for r in range(1, len(RANGES)):
             second_layer(r, woven[r])

@@ -171,12 +171,6 @@ def tile_picked_dconv_none_e_kernel(tc, xT, w1, w2, taps, offs, out):
         quantize_w1(0, 3, 0)
         quantize_w1(1, 3)
         late_term(3)
-        near = keep.tile([P, S], F32, name="near")
-        for a, b in halves:
-            nc.scalar.activation(out=near[:, a:b], in_=h[3][:, a:b], func=COPY, scale=tap[3][:, 1:2])
-            nc.gpsimd.tensor_tensor(
-                out=mid[:, 3, PAD + a : PAD + b], in0=near[:, a:b], in1=late[:, 3, PAD + a - 1 : PAD + b - 1], op=ADD
-            )
         w2_bf = keep.tile([P, N * PACK], BF16, name="w2_bf", align_bytes=64)
         nc.scalar.copy(
             out=w2_bf[:].rearrange("p (c i j) -> p c j i", i=4, j=PACK),
@@ -241,15 +235,17 @@ def tile_picked_dconv_none_e_kernel(tc, xT, w1, w2, taps, offs, out):
             )
             result = keep.tile([P, b - a], F32, name=f"result{r}")
             nc.scalar.copy(out=result[:], in_=acc[:])
-            nc.sync.dma_start(out=out[:, a:b], in_=result[:])
+            queue = nc.scalar if r == len(RANGES) - 1 else nc.sync
+            queue.dma_start(out=out[:, a:b], in_=result[:])
 
         first_sum(0)
         first_sum(1)
         second_sum(0, *halves[0])
         first_sum(2)
         second_sum(1, *halves[0])
-        second_sum(0, *halves[1])
+        first_sum(3)
         second_sum(2, *halves[0])
+        second_sum(0, *halves[1])
         second_sum(3, *halves[0])
         woven = [weave(0)]
         second_sum(1, *halves[1])

@@ -21,7 +21,11 @@ PACK = 4
 K_PASS = P * PACK
 PASSES = K // K_PASS
 PAD = 8
-SPARE = 8
+HALF = S // 2
+X_CHUNKS = ((0, 0, 512), (0, 512, 768), (0, 768, 1024), (1, 0, 512), (1, 512, 768), (1, 768, 1024))
+W_CHUNK = H // 2
+M_CHUNK = W_CHUNK // PACK
+PLANE_STEP = 4
 RANGES = ((0, 256), (256, 384), (384, 512))
 
 
@@ -29,203 +33,186 @@ def tile_picked_dconv_none_e_kernel(tc, xT, w1, w2, taps, offs, out):
     nc = tc.nc
     with ExitStack() as ctx:
         keep = ctx.enter_context(tc.tile_pool(name="keep", bufs=1))
-        placed = ctx.enter_context(tc.tile_pool(name="placed", bufs=1))
         psum = ctx.enter_context(tc.psum_pool(name="psum", bufs=1))
 
         offsets = keep.tile([P, S // 16], U16, name="offsets")
-        tap_pair = [keep.tile([P, 2 * D], F32, name=f"tap{a}") for a in range(2)]
-        tap = [tap_pair[t // 2][:, (t % 2) * D : (t % 2 + 1) * D] for t in range(PACK)]
-        x_raw = [keep.tile([P, 2, T], F32, name=f"x_raw{i}") for i in range(2 * PASSES)]
-        w1_raw = [keep.tile([P, PACK, H], F32, name=f"w1_raw{g}") for g in range(PASSES)]
+        tap = keep.tile([P, PACK * D], F32, name="tap")
+        x_raw = [keep.tile([P, PACK, b - a], F32, name=f"x_raw{i}") for i, (g, a, b) in enumerate(X_CHUNKS)]
+        w1_raw = [[keep.tile([P, PACK, W_CHUNK], F32, name=f"w1_raw{g}{c}") for c in range(2)] for g in range(PASSES)]
         w2_raw = keep.tile([P, PACK, N], F32, name="w2_raw")
 
-        x_rows = xT.rearrange("(g p u e) t -> g u p e t", g=PASSES, p=P, u=2, e=2)
-        w1_rows = w1.rearrange("(g p j) h -> g p j h", g=PASSES, j=PACK)
-        nc.sync.dma_start(out=x_raw[0][:], in_=x_rows[0, 0])
-        nc.sync.dma_start(offsets[:], offs)
-        for i in range(1, 2 * PASSES):
-            nc.sync.dma_start(out=x_raw[i][:], in_=x_rows[i // 2, i % 2])
-        for g in range(PASSES):
-            nc.sync.dma_start(out=w1_raw[g][:], in_=w1_rows[g])
-        tap_rows = taps.rearrange("(b a r e) d -> a b r (e d)", a=2, r=8, e=2)
-        for a in range(2):
-            nc.sync.dma_start(out=tap_pair[a][:], in_=tap_rows[a])
-        w2_rows = w2.rearrange("(b a r e) n -> a b r (e n)", a=2, r=8, e=2)
-        for a in range(2):
-            nc.sync.dma_start(out=w2_raw[:, 2 * a : 2 * a + 2, :].rearrange("p e n -> p (e n)"), in_=w2_rows[a])
+        x_rows = xT.rearrange("(g p j) t -> g p j t", g=PASSES, j=PACK)
+        w1_rows = w1.rearrange("(g p j) (c h) -> g c p j h", g=PASSES, j=PACK, c=2)
+        for i, (g, a, b) in enumerate(X_CHUNKS):
+            nc.sync.dma_start(out=x_raw[i][:], in_=x_rows[g, :, :, a:b])
+            if i == 0:
+                nc.sync.dma_start(offsets[:], offs)
+        for i in range(2 * PASSES):
+            nc.sync.dma_start(out=w1_raw[i // 2][i % 2][:], in_=w1_rows[i // 2, i % 2])
+        nc.sync.dma_start(out=tap[:], in_=taps.rearrange("(p t) d -> p (t d)", t=PACK))
+        nc.sync.dma_start(out=w2_raw[:], in_=w2.rearrange("(p j) n -> p j n", j=PACK))
 
         late = keep.tile([P, PACK, PAD + S], F32, name="late")
-        mid = keep.tile([P, PACK, PAD + S], F32, name="mid")
-        nc.vector.memset(mid[:, :, 0:PAD], 0.0)
+        mid = keep.tile([P, PACK, 2 * PAD + S], F32, name="mid")
+        planes = keep.tile([P, T], U8, name="planes", align_bytes=64)
+        nc.vector.memset(planes[:].bitcast(I32), 0)
+        nc.vector.memset(mid[:, :, 0 : PAD + 1], 0.0)
         nc.scalar.activation(out=late[:, :, 0:PAD], in_=mid[:, :, 0:PAD], func=COPY)
 
-        early = keep.tile([P, 2 * 2 * T], BF16, name="early", align_bytes=64)
-        third = keep.tile([P, 2 * T], BF16, name="third", align_bytes=64)
-        fourth = keep.tile([P, 2 * T], BF16, name="fourth", align_bytes=64)
-        picked0 = keep.tile([P, S * PACK], BF16, name="picked0", align_bytes=64)
-        picked1 = keep.tile([P, S * PACK], BF16, name="picked1", align_bytes=64)
-        nc.vector.memset(early[:, 2 * T : 2 * (T + SPARE)], 0.0)
-        pairs = [early[:, : 2 * T], early[:, 2 * T :], third[:], fourth[:]]
-        windows = [early[:, : 2 * (T + SPARE)]] + pairs[1:]
-        picked = [picked0[:], picked1[:]]
-        x_q = {}
+        x_bf = [keep.tile([P, (b - a) * PACK], BF16, name=f"x_bf{i}", align_bytes=64) for i, (g, a, b) in enumerate(X_CHUNKS)]
+        words = [keep.tile([P, T], U32, name=f"words{g}", align_bytes=64) for g in range(PASSES)]
+        picked = [keep.tile([P, S], U32, name=f"picked{g}", align_bytes=64) for g in range(PASSES)]
+        picked_planes = keep.tile([P, S], U8, name="picked_planes", align_bytes=64)
 
-        def x_tiles(g, offset):
-            if offset is None:
-                codes = keep.tile([P, S], U32, name=f"x_codes{g}", align_bytes=64)
-            else:
-                codes = placed.tile([P, S], U32, name=f"x_codes{g}", align_bytes=64, offset=offset)
-            scales = keep.tile([P, S], U8, name=f"x_scales{g}", align_bytes=64)
-            x_q[g] = (codes, scales)
-
-        h = [psum.tile([P, S], F32, name=f"h{t}") for t in range(PACK)]
-        w1_bf = {}
-
-        def round_x(i, a, b, engine):
-            dst = pairs[i].rearrange("p (t e) -> p t e", e=2)[:, a:b, :]
-            src = x_raw[i][:].rearrange("p e t -> p t e")[:, a:b, :]
-            if engine == "vector":
+        def round_x(i, a, b, on_vector):
+            dst = x_bf[i][:, a * PACK : b * PACK].rearrange("p (c i j) -> p c j i", i=4, j=PACK)
+            src = x_raw[i][:, :, a:b].rearrange("p j (c i) -> p c j i", i=4)
+            if on_vector:
                 nc.vector.tensor_copy(out=dst, in_=src)
-            elif engine == "scalar":
-                nc.scalar.copy(out=dst, in_=src)
             else:
-                nc.gpsimd.tensor_scalar(out=dst, in0=src, scalar1=1.0, scalar2=0.0, op0=MULT, op1=ADD)
+                nc.scalar.activation(out=dst, in_=src, func=COPY)
 
-        def pick(i, a, b):
-            g, u = divmod(i, 2)
-            nc.vector.tensor_copy(
-                out=picked[g].bitcast(U32).rearrange("p (n u) -> p n u", u=2)[:, a:b, u],
-                in_=windows[i].bitcast(U32).indirect(offsets[:, a // 16 : b // 16]),
-            )
-
-        def quantize_x(g, a, b):
-            codes, scales = x_q[g]
+        def quantize_x(i):
+            g, a, b = X_CHUNKS[i]
             nc.vector.quantize_mx(
-                out=codes[:, a:b].bitcast(FP8X4), scales=scales[:, a:b], in_=picked[g][:, a * PACK : b * PACK]
+                out=words[g][:, a:b].bitcast(FP8X4),
+                scales=planes[PLANE_STEP * g :, a:b],
+                in_=x_bf[i][:],
             )
 
-        def round_w1(g, t, bf, on_vector):
-            src = w1_raw[g][:].rearrange("p j (b a c i e) -> p a e b c j i", a=2, c=4, i=2, e=2)[:, t // 2, t % 2]
-            dst = bf.rearrange("p (b c i j) -> p b c j i", c=4, i=2, j=PACK)
+        def pick(dst, window):
+            nc.vector.tensor_copy(out=dst[:], in_=window[:].indirect(offsets[:]))
+
+        w1_bf = [keep.tile([P, PACK, P, PACK], BF16, name=f"w1_bf{g}", align_bytes=64, tag=f"w_bf{g}") for g in range(PASSES)]
+        w1_codes = [keep.tile([P, PACK, P], U32, name=f"w1_codes{g}", align_bytes=64) for g in range(PASSES)]
+        w1_scales = [keep.tile([P, PACK, P], U8, name=f"w1_scales{g}", align_bytes=64) for g in range(PASSES)]
+
+        def round_w1(g, c, a, b, on_vector):
+            m0 = c * M_CHUNK
+            dst = w1_bf[g][:, :, m0 + a : m0 + b, :].rearrange("p t m j -> p m j t")
+            src = w1_raw[g][c][:, :, a * PACK : b * PACK].rearrange("p j (m t) -> p m j t", t=PACK)
             if on_vector:
                 nc.vector.tensor_copy(out=dst, in_=src)
             else:
                 nc.scalar.copy(out=dst, in_=src)
-            w1_bf[g, t] = bf
 
-        def fresh(name, offset=None):
-            if offset is None:
-                tile = keep.tile([P, K_PASS], BF16, name=name, align_bytes=64)
-            else:
-                tile = placed.tile([P, K_PASS], BF16, name=name, align_bytes=64, offset=offset)
-            return tile[:]
-
-        def quantize_w1(g, t, offset=None):
-            if offset is None:
-                codes = keep.tile([P, P], U32, name=f"w1_codes{g}{t}", align_bytes=64)
-            else:
-                codes = placed.tile([P, P], U32, name=f"w1_codes{g}{t}", align_bytes=64, offset=offset)
-            scales = keep.tile([P, P], U8, name=f"w1_scales{g}{t}", align_bytes=64)
-            nc.vector.quantize_mx(out=codes[:].bitcast(FP8X4), scales=scales[:], in_=w1_bf[g, t])
-            nc.tensor.matmul_mx(
-                out=h[t][:],
-                lhsT=codes[:].bitcast(FP8X4),
-                lhsT_scale=scales[:],
-                rhs=x_q[g][0][:].bitcast(FP8X4),
-                rhs_scale=x_q[g][1][:],
-                start=(g == 0),
-                stop=(g == PASSES - 1),
+        def quantize_w1(g, ta, tb):
+            nc.vector.quantize_mx(
+                out=w1_codes[g][:, ta:tb, :].rearrange("p t m -> p (t m)").bitcast(FP8X4),
+                scales=w1_scales[g][:, ta:tb, :].rearrange("p t m -> p (t m)"),
+                in_=w1_bf[g][:, ta:tb].rearrange("p t m j -> p (t m j)"),
             )
 
-        def late_term(t):
-            nc.scalar.activation(out=late[:, t, PAD:], in_=h[t][:], func=COPY, scale=tap[t][:, 2:3])
+        h = [[psum.tile([P, HALF], F32, name=f"h{t}{hf}", tag=f"bank{t}{hf}") for hf in range(2)] for t in range(PACK)]
 
-        for i in range(2):
-            round_x(i, 640, T, "scalar")
-            round_x(i, 0, 640, "vector")
-            pick(i, 0, S)
-        x_tiles(0, None)
-        quantize_x(0, 0, S)
-        round_x(2, 0, 800, "scalar")
-        round_x(2, 800, T, "gpsimd")
-        round_x(3, 0, 608, "scalar")
-        round_x(3, 608, T, "gpsimd")
-        pick(2, 0, S)
-        pick(3, 0, S)
-        halves = ((0, S // 2), (S // 2, S))
-        round_w1(0, 0, fresh("w1_bf00", 2048), False)
-        for t in range(1, PACK):
-            round_w1(0, t, fresh(f"w1_bf0{t}"), False)
-        quantize_w1(0, 0)
-        x_tiles(1, 2048)
-        quantize_x(1, 0, S)
-        quantize_w1(0, 1)
-        quantize_w1(0, 2)
-        round_w1(1, 0, fresh("w1_bf10", 0), False)
-        round_w1(1, 1, fresh("w1_bf11"), True)
-        round_w1(1, 2, fresh("w1_bf12"), True)
-        round_w1(1, 3, fresh("w1_bf13"), False)
-        for t in range(PACK - 1):
-            quantize_w1(1, t)
-            late_term(t)
-        quantize_w1(0, 3, 0)
-        quantize_w1(1, 3)
-        late_term(3)
+        def first_layer(g, t, hf):
+            nc.tensor.matmul_mx(
+                out=h[t][hf][:],
+                lhsT=w1_codes[g][:, t, :].bitcast(FP8X4),
+                lhsT_scale=w1_scales[g][:, t, :],
+                rhs=picked[g][:, hf * HALF : (hf + 1) * HALF].bitcast(FP8X4),
+                rhs_scale=picked_planes[PLANE_STEP * g :, hf * HALF : (hf + 1) * HALF],
+                start=(g == hf),
+                stop=(g != hf),
+            )
+
+        for i, on_vector in enumerate((336, 168, 168, 256)):
+            g, a, b = X_CHUNKS[i]
+            round_x(i, on_vector, b - a, False)
+            round_x(i, 0, on_vector, True)
+            quantize_x(i)
+            if i == 2:
+                pick(picked[0], words[0])
+        round_x(4, 0, 256, False)
+        round_x(5, 168, 256, False)
+        round_x(5, 0, 168, True)
+        quantize_x(4)
+        quantize_x(5)
+        round_w1(0, 0, 0, M_CHUNK, False)
+        pick(picked_planes, planes)
+        pick(picked[1], words[1])
+        round_w1(0, 1, 0, M_CHUNK, False)
+        quantize_w1(0, 0, 2)
+        quantize_w1(0, 2, 4)
+        for t in range(PACK):
+            first_layer(0, t, 0)
+        round_w1(1, 0, 0, M_CHUNK, False)
+        round_w1(1, 1, 40, M_CHUNK, False)
+        round_w1(1, 1, 0, 40, True)
+        for t in range(PACK):
+            quantize_w1(1, t, t + 1)
+            first_layer(1, t, 0)
+        for t in range(PACK):
+            first_layer(1, t, 1)
+            first_layer(0, t, 1)
+
         w2_bf = keep.tile([P, N * PACK], BF16, name="w2_bf", align_bytes=64)
-        nc.scalar.copy(
+        w2_codes = keep.tile([P, N], U32, name="w2_codes", align_bytes=64)
+        w2_scales = keep.tile([P, N], U8, name="w2_scales", align_bytes=64)
+        nc.vector.tensor_copy(
             out=w2_bf[:].rearrange("p (c i j) -> p c j i", i=4, j=PACK),
             in_=w2_raw[:].rearrange("p j (c i) -> p c j i", i=4),
         )
-        w2_codes = keep.tile([P, N], U32, name="w2_codes", align_bytes=64)
-        w2_scales = keep.tile([P, N], U8, name="w2_scales", align_bytes=64)
-        nc.vector.quantize_mx(out=w2_codes[:].bitcast(FP8X4), scales=w2_scales[:], in_=w2_bf[:])
 
-        z_tiles = []
-        for half in range(2):
-            z = keep.tile([P, PACK, S // 2], BF16, name=f"z{half}", align_bytes=64)
-            z_tiles.append(z)
+        z = [keep.tile([P, PACK, HALF], BF16, name=f"z{hf}", align_bytes=64) for hf in range(2)]
 
-        def first_sum(t):
+        def late_term(t, hf):
+            a = PAD + hf * HALF
+            nc.scalar.activation(out=late[:, t, a : a + HALF], in_=h[t][hf][:], func=COPY, scale=tap[:, D * t + 2 : D * t + 3])
+
+        def first_sum(t, hf):
+            a = PAD + hf * HALF
             nc.vector.scalar_tensor_tensor(
-                out=mid[:, t, PAD:],
-                in0=h[t][:],
-                scalar=tap[t][:, 1:2],
-                in1=late[:, t, PAD - 1 : PAD + S - 1],
+                out=mid[:, t, a + 1 : a + HALF + 1],
+                in0=h[t][hf][:],
+                scalar=tap[:, D * t + 1 : D * t + 2],
+                in1=late[:, t, a - 1 : a + HALF - 1],
                 op0=MULT,
                 op1=ADD,
             )
 
         def second_sum(t, a, b):
-            half, a0 = divmod(a, S // 2)
+            hf, a0 = divmod(a, HALF)
             nc.vector.scalar_tensor_tensor(
-                out=z_tiles[half][:, t, a0 : a0 + b - a],
-                in0=h[t][:, a:b],
-                scalar=tap[t][:, 0:1],
-                in1=mid[:, t, PAD + a - 1 : PAD + b - 1],
+                out=z[hf][:, t, a0 : a0 + b - a],
+                in0=h[t][hf][:, a0 : a0 + b - a],
+                scalar=tap[:, D * t : D * t + 1],
+                in1=mid[:, t, PAD + a : PAD + b],
                 op0=MULT,
                 op1=ADD,
             )
 
+        woven = [keep.tile([P, (b - a) * PACK], BF16, name=f"woven{r}", align_bytes=64) for r, (a, b) in enumerate(RANGES)]
+
         def weave(r):
             a, b = RANGES[r]
-            half, a0 = divmod(a, S // 2)
-            woven = keep.tile([P, (b - a) * PACK], BF16, name=f"woven{r}", align_bytes=64)
-            dst = woven[:].rearrange("p (c i t) -> p c t i", i=4, t=PACK)
-            src = z_tiles[half][:, :, a0 : a0 + b - a].rearrange("p t (c i) -> p c t i", i=4)
-            if r == len(RANGES) - 1:
-                nc.vector.tensor_copy(out=dst, in_=src)
-            else:
-                nc.scalar.copy(out=dst, in_=src)
-            return woven
+            hf, a0 = divmod(a, HALF)
+            dst = woven[r][:].rearrange("p (c i t) -> p c t i", i=4, t=PACK)
+            src = z[hf][:, :, a0 : a0 + b - a].rearrange("p t (c i) -> p c t i", i=4)
+            nc.scalar.copy(out=dst, in_=src)
 
-        def second_layer(r, woven):
+        last_a, last_b = RANGES[-1]
+        early = keep.tile([P, PACK, last_b - last_a], F32, name="early")
+
+        def early_term(t):
+            nc.scalar.activation(out=early[:, t, :], in_=h[t][1][:, last_a - HALF :], func=COPY, scale=tap[:, D * t : D * t + 1])
+
+        def woven_sum():
+            nc.vector.tensor_tensor(
+                out=woven[-1][:].rearrange("p (c i t) -> p c t i", i=4, t=PACK),
+                in0=early[:].rearrange("p t (c i) -> p c t i", i=4),
+                in1=mid[:, :, PAD + last_a : PAD + last_b].rearrange("p t (c i) -> p c t i", i=4),
+                op=ADD,
+            )
+
+        def second_layer(r):
             a, b = RANGES[r]
             codes = keep.tile([P, b - a], U32, name=f"z_codes{r}", align_bytes=64)
             scales = keep.tile([P, b - a], U8, name=f"z_scales{r}", align_bytes=64)
-            nc.vector.quantize_mx(out=codes[:].bitcast(FP8X4), scales=scales[:], in_=woven[:])
-            acc = psum.tile([P, b - a], F32, name=f"acc{r}")
+            nc.vector.quantize_mx(out=codes[:].bitcast(FP8X4), scales=scales[:], in_=woven[r][:])
+            acc = psum.tile([P, HALF], F32, name=f"acc{r}", tag=f"bank{r}0")
             nc.tensor.matmul_mx(
-                out=acc[:],
+                out=acc[:, : b - a],
                 lhsT=w2_codes[:].bitcast(FP8X4),
                 lhsT_scale=w2_scales[:],
                 rhs=codes[:].bitcast(FP8X4),
@@ -234,26 +221,29 @@ def tile_picked_dconv_none_e_kernel(tc, xT, w1, w2, taps, offs, out):
                 stop=True,
             )
             result = keep.tile([P, b - a], F32, name=f"result{r}")
-            nc.scalar.copy(out=result[:], in_=acc[:])
+            nc.scalar.copy(out=result[:], in_=acc[:, : b - a])
             queue = nc.scalar if r == len(RANGES) - 1 else nc.sync
             queue.dma_start(out=out[:, a:b], in_=result[:])
 
-        first_sum(0)
-        first_sum(1)
-        second_sum(0, *halves[0])
-        first_sum(2)
-        second_sum(1, *halves[0])
-        first_sum(3)
-        second_sum(2, *halves[0])
-        second_sum(0, *halves[1])
-        second_sum(3, *halves[0])
-        woven = [weave(0)]
-        second_sum(1, *halves[1])
-        second_sum(2, *halves[1])
-        second_sum(3, *RANGES[1])
-        woven.append(weave(1))
-        second_sum(3, *RANGES[2])
-        second_layer(0, woven[0])
-        woven.append(weave(2))
-        for r in range(1, len(RANGES)):
-            second_layer(r, woven[r])
+        for hf in range(2):
+            for t in range(PACK):
+                late_term(t, hf)
+        first_sum(0, 0)
+        nc.vector.quantize_mx(out=w2_codes[:].bitcast(FP8X4), scales=w2_scales[:], in_=w2_bf[:])
+        for t in range(1, PACK):
+            first_sum(t, 0)
+            second_sum(t - 1, 0, HALF)
+        first_sum(0, 1)
+        second_sum(PACK - 1, 0, HALF)
+        weave(0)
+        for t in range(1, PACK):
+            first_sum(t, 1)
+            second_sum(t - 1, *RANGES[1])
+        second_sum(PACK - 1, *RANGES[1])
+        for t in range(PACK):
+            early_term(t)
+        weave(1)
+        second_layer(0)
+        woven_sum()
+        second_layer(1)
+        second_layer(2)

@@ -22,9 +22,7 @@ K_PASS = P * PACK
 PASSES = K // K_PASS
 PAD = 8
 HALF = S // 2
-X_CHUNKS = ((0, 0, 512), (0, 512, 768), (0, 768, 1024), (1, 0, 512), (1, 512, 768), (1, 768, 1024))
-W_CHUNK = H // 2
-M_CHUNK = W_CHUNK // PACK
+X_CHUNKS = ((0, 0, 1024), (1, 0, 512), (1, 512, 1024))
 PLANE_STEP = 4
 RANGES = ((0, 256), (256, 384), (384, 512))
 
@@ -38,17 +36,17 @@ def tile_picked_dconv_none_e_kernel(tc, xT, w1, w2, taps, offs, out):
         offsets = keep.tile([P, S // 16], U16, name="offsets")
         tap = keep.tile([P, PACK * D], F32, name="tap")
         x_raw = [keep.tile([P, PACK, b - a], F32, name=f"x_raw{i}") for i, (g, a, b) in enumerate(X_CHUNKS)]
-        w1_raw = [[keep.tile([P, PACK, W_CHUNK], F32, name=f"w1_raw{g}{c}") for c in range(2)] for g in range(PASSES)]
+        w1_raw = [keep.tile([P, PACK, H], F32, name=f"w1_raw{g}", tag=f"raw{g}", align_bytes=64) for g in range(PASSES)]
         w2_raw = keep.tile([P, PACK, N], F32, name="w2_raw")
 
         x_rows = xT.rearrange("(g p j) t -> g p j t", g=PASSES, j=PACK)
-        w1_rows = w1.rearrange("(g p j) (c h) -> g c p j h", g=PASSES, j=PACK, c=2)
+        w1_rows = w1.rearrange("(g p j) h -> g p j h", g=PASSES, j=PACK)
         for i, (g, a, b) in enumerate(X_CHUNKS):
             nc.sync.dma_start(out=x_raw[i][:], in_=x_rows[g, :, :, a:b])
             if i == 0:
                 nc.sync.dma_start(offsets[:], offs)
-        for i in range(2 * PASSES):
-            nc.sync.dma_start(out=w1_raw[i // 2][i % 2][:], in_=w1_rows[i // 2, i % 2])
+        for g in range(PASSES):
+            nc.sync.dma_start(out=w1_raw[g][:], in_=w1_rows[g])
         nc.sync.dma_start(out=tap[:], in_=taps.rearrange("(p t) d -> p (t d)", t=PACK))
         nc.sync.dma_start(out=w2_raw[:], in_=w2.rearrange("(p j) n -> p j n", j=PACK))
 
@@ -59,89 +57,97 @@ def tile_picked_dconv_none_e_kernel(tc, xT, w1, w2, taps, offs, out):
         nc.vector.memset(mid[:, :, 0 : PAD + 1], 0.0)
         nc.scalar.activation(out=late[:, :, 0:PAD], in_=mid[:, :, 0:PAD], func=COPY)
 
-        x_bf = [keep.tile([P, (b - a) * PACK], BF16, name=f"x_bf{i}", align_bytes=64) for i, (g, a, b) in enumerate(X_CHUNKS)]
+        x_bf = [keep.tile([P, T * PACK], BF16, name=f"x_bf{g}", align_bytes=64) for g in range(PASSES)]
         words = [keep.tile([P, T], U32, name=f"words{g}", align_bytes=64) for g in range(PASSES)]
         picked = [keep.tile([P, S], U32, name=f"picked{g}", align_bytes=64) for g in range(PASSES)]
-        picked_planes = keep.tile([P, S], U8, name="picked_planes", align_bytes=64)
+        picked_planes = [keep.tile([P, HALF], U8, name="picked_planes0", align_bytes=64)]
 
         def round_x(i, a, b, on_vector):
-            dst = x_bf[i][:, a * PACK : b * PACK].rearrange("p (c i j) -> p c j i", i=4, j=PACK)
-            src = x_raw[i][:, :, a:b].rearrange("p j (c i) -> p c j i", i=4)
+            g, first, last = X_CHUNKS[i]
+            dst = x_bf[g][:, a * PACK : b * PACK].rearrange("p (c i j) -> p c j i", i=4, j=PACK)
+            src = x_raw[i][:, :, a - first : b - first].rearrange("p j (c i) -> p c j i", i=4)
             if on_vector:
                 nc.vector.tensor_copy(out=dst, in_=src)
             else:
                 nc.scalar.activation(out=dst, in_=src, func=COPY)
 
-        def quantize_x(i):
-            g, a, b = X_CHUNKS[i]
+        def quantize_x(g, a, b):
             nc.vector.quantize_mx(
                 out=words[g][:, a:b].bitcast(FP8X4),
                 scales=planes[PLANE_STEP * g :, a:b],
-                in_=x_bf[i][:],
+                in_=x_bf[g][:, a * PACK : b * PACK],
             )
 
-        def pick(dst, window):
-            nc.vector.tensor_copy(out=dst[:], in_=window[:].indirect(offsets[:]))
+        def pick(dst, window, a, b):
+            nc.vector.tensor_copy(out=dst[:], in_=window[:].indirect(offsets[:, a // 16 : b // 16]))
 
         w1_bf = [keep.tile([P, PACK, P, PACK], BF16, name=f"w1_bf{g}", align_bytes=64, tag=f"w_bf{g}") for g in range(PASSES)]
-        w1_codes = [keep.tile([P, PACK, P], U32, name=f"w1_codes{g}", align_bytes=64) for g in range(PASSES)]
-        w1_scales = [keep.tile([P, PACK, P], U8, name=f"w1_scales{g}", align_bytes=64) for g in range(PASSES)]
+        w1_q = {}
 
-        def round_w1(g, c, a, b, on_vector):
-            m0 = c * M_CHUNK
-            dst = w1_bf[g][:, :, m0 + a : m0 + b, :].rearrange("p t m j -> p m j t")
-            src = w1_raw[g][c][:, :, a * PACK : b * PACK].rearrange("p j (m t) -> p m j t", t=PACK)
+        def round_w1(g, ta, on_vector):
+            dst = w1_bf[g][:, ta : ta + 2].rearrange("p t m j -> p m j t")
+            src = w1_raw[g][:].rearrange("p j (m t) -> p m j t", t=PACK)[:, :, :, ta : ta + 2]
             if on_vector:
                 nc.vector.tensor_copy(out=dst, in_=src)
             else:
                 nc.scalar.copy(out=dst, in_=src)
 
-        def quantize_w1(g, ta, tb):
+        def quantize_w1(g, ta, tb, tag=""):
+            codes = keep.tile([P, (tb - ta) * P], U32, name=f"w1_codes{g}{ta}", align_bytes=64, tag=tag)
+            scales = keep.tile([P, (tb - ta) * P], U8, name=f"w1_scales{g}{ta}", align_bytes=64)
             nc.vector.quantize_mx(
-                out=w1_codes[g][:, ta:tb, :].rearrange("p t m -> p (t m)").bitcast(FP8X4),
-                scales=w1_scales[g][:, ta:tb, :].rearrange("p t m -> p (t m)"),
+                out=codes[:].bitcast(FP8X4),
+                scales=scales[:],
                 in_=w1_bf[g][:, ta:tb].rearrange("p t m j -> p (t m j)"),
             )
+            for t in range(ta, tb):
+                cols = slice((t - ta) * P, (t - ta + 1) * P)
+                w1_q[g, t] = (codes[:, cols], scales[:, cols])
 
         h = [[psum.tile([P, HALF], F32, name=f"h{t}{hf}", tag=f"bank{t}{hf}") for hf in range(2)] for t in range(PACK)]
 
         def first_layer(g, t, hf):
             nc.tensor.matmul_mx(
                 out=h[t][hf][:],
-                lhsT=w1_codes[g][:, t, :].bitcast(FP8X4),
-                lhsT_scale=w1_scales[g][:, t, :],
+                lhsT=w1_q[g, t][0].bitcast(FP8X4),
+                lhsT_scale=w1_q[g, t][1],
                 rhs=picked[g][:, hf * HALF : (hf + 1) * HALF].bitcast(FP8X4),
-                rhs_scale=picked_planes[PLANE_STEP * g :, hf * HALF : (hf + 1) * HALF],
+                rhs_scale=picked_planes[hf][PLANE_STEP * g :, :],
                 start=(g == hf),
                 stop=(g != hf),
             )
 
-        for i, on_vector in enumerate((336, 168, 168, 256)):
-            g, a, b = X_CHUNKS[i]
-            round_x(i, on_vector, b - a, False)
-            round_x(i, 0, on_vector, True)
-            quantize_x(i)
-            if i == 2:
-                pick(picked[0], words[0])
-        round_x(4, 0, 256, False)
-        round_x(5, 168, 256, False)
-        round_x(5, 0, 168, True)
-        quantize_x(4)
-        quantize_x(5)
-        round_w1(0, 0, 0, M_CHUNK, False)
-        pick(picked_planes, planes)
-        pick(picked[1], words[1])
-        round_w1(0, 1, 0, M_CHUNK, False)
+        round_x(0, 640, 1024, False)
+        round_x(0, 0, 512, True)
+        round_x(0, 512, 640, True)
+        quantize_x(0, 0, 512)
+        quantize_x(0, 512, 1024)
+        pick(picked[0], words[0], 0, S)
+        round_x(1, 0, 256, False)
+        round_x(1, 256, 512, False)
+        quantize_x(1, 0, 256)
+        round_x(2, 832, 1024, False)
+        round_x(2, 512, 768, True)
+        round_x(2, 768, 832, True)
+        quantize_x(1, 256, 768)
+        quantize_x(1, 768, 1024)
+        pick(picked_planes[0], planes, 0, HALF)
+        pick(picked[1], words[1], 0, S)
+        round_w1(0, 0, False)
+        round_w1(0, 2, False)
         quantize_w1(0, 0, 2)
-        quantize_w1(0, 2, 4)
-        for t in range(PACK):
+        for t in range(2):
             first_layer(0, t, 0)
-        round_w1(1, 0, 0, M_CHUNK, False)
-        round_w1(1, 1, 40, M_CHUNK, False)
-        round_w1(1, 1, 0, 40, True)
+        round_w1(1, 0, True)
+        round_w1(1, 2, False)
+        quantize_w1(0, 2, 4)
+        for t in range(2, PACK):
+            first_layer(0, t, 0)
         for t in range(PACK):
             quantize_w1(1, t, t + 1)
             first_layer(1, t, 0)
+        picked_planes.append(keep.tile([P, HALF], U8, name="picked_planes1", tag="raw1", align_bytes=64))
+        pick(picked_planes[1], planes, HALF, S)
         for t in range(PACK):
             first_layer(1, t, 1)
             first_layer(0, t, 1)
@@ -149,7 +155,7 @@ def tile_picked_dconv_none_e_kernel(tc, xT, w1, w2, taps, offs, out):
         w2_bf = keep.tile([P, N * PACK], BF16, name="w2_bf", align_bytes=64)
         w2_codes = keep.tile([P, N], U32, name="w2_codes", align_bytes=64)
         w2_scales = keep.tile([P, N], U8, name="w2_scales", align_bytes=64)
-        nc.vector.tensor_copy(
+        nc.scalar.copy(
             out=w2_bf[:].rearrange("p (c i j) -> p c j i", i=4, j=PACK),
             in_=w2_raw[:].rearrange("p j (c i) -> p c j i", i=4),
         )

@@ -24,6 +24,7 @@ PAD = 8
 HALF = S // 2
 X_CHUNKS = ((0, 0, 1024), (1, 0, 512), (1, 512, 1024))
 PLANE_STEP = 4
+W1_SLOTS = ((0, 0), (0, 1), (1, 0), (1, 1), (0, 2), (0, 3), (1, 2), (1, 3))
 RANGES = ((0, 256), (256, 384), (384, 512))
 
 
@@ -52,7 +53,7 @@ def tile_picked_dconv_none_e_kernel(tc, xT, w1, w2, taps, offs, out):
 
         late = keep.tile([P, PACK, PAD + S], F32, name="late")
         mid = keep.tile([P, PACK, 2 * PAD + S], F32, name="mid")
-        planes = keep.tile([P, T], U8, name="planes", align_bytes=64)
+        planes = keep.tile([P, T], U8, name="planes", tag="planes", align_bytes=64)
         nc.vector.memset(planes[:].bitcast(I32), 0)
         nc.vector.memset(mid[:, :, 0 : PAD + 1], 0.0)
         nc.scalar.activation(out=late[:, :, 0:PAD], in_=mid[:, :, 0:PAD], func=COPY)
@@ -81,28 +82,29 @@ def tile_picked_dconv_none_e_kernel(tc, xT, w1, w2, taps, offs, out):
         def pick(dst, window, a, b):
             nc.vector.tensor_copy(out=dst[:], in_=window[:].indirect(offsets[:, a // 16 : b // 16]))
 
-        w1_bf = [keep.tile([P, PACK, P, PACK], BF16, name=f"w1_bf{g}", align_bytes=64, tag=f"w_bf{g}") for g in range(PASSES)]
+        w1_bf = keep.tile([P, len(W1_SLOTS), P, PACK], BF16, name="w1_bf", align_bytes=64)
         w1_q = {}
 
         def round_w1(g, ta, on_vector):
-            dst = w1_bf[g][:, ta : ta + 2].rearrange("p t m j -> p m j t")
+            first = W1_SLOTS.index((g, ta))
+            dst = w1_bf[:, first : first + 2].rearrange("p t m j -> p m j t")
             src = w1_raw[g][:].rearrange("p j (m t) -> p m j t", t=PACK)[:, :, :, ta : ta + 2]
             if on_vector:
                 nc.vector.tensor_copy(out=dst, in_=src)
             else:
                 nc.scalar.copy(out=dst, in_=src)
 
-        def quantize_w1(g, ta, tb, tag=""):
-            codes = keep.tile([P, (tb - ta) * P], U32, name=f"w1_codes{g}{ta}", align_bytes=64, tag=tag)
-            scales = keep.tile([P, (tb - ta) * P], U8, name=f"w1_scales{g}{ta}", align_bytes=64)
+        def quantize_w1(first, last):
+            codes = keep.tile([P, (last - first) * P], U32, name=f"w1_codes{first}", align_bytes=64)
+            scales = keep.tile([P, (last - first) * P], U8, name=f"w1_scales{first}", align_bytes=64)
             nc.vector.quantize_mx(
                 out=codes[:].bitcast(FP8X4),
                 scales=scales[:],
-                in_=w1_bf[g][:, ta:tb].rearrange("p t m j -> p (t m j)"),
+                in_=w1_bf[:, first:last].rearrange("p t m j -> p (t m j)"),
             )
-            for t in range(ta, tb):
-                cols = slice((t - ta) * P, (t - ta + 1) * P)
-                w1_q[g, t] = (codes[:, cols], scales[:, cols])
+            for slot in range(first, last):
+                cols = slice((slot - first) * P, (slot - first + 1) * P)
+                w1_q[W1_SLOTS[slot]] = (codes[:, cols], scales[:, cols])
 
         h = [[psum.tile([P, HALF], F32, name=f"h{t}{hf}", tag=f"bank{t}{hf}") for hf in range(2)] for t in range(PACK)]
 
@@ -135,30 +137,26 @@ def tile_picked_dconv_none_e_kernel(tc, xT, w1, w2, taps, offs, out):
         pick(picked[1], words[1], 0, S)
         round_w1(0, 0, False)
         round_w1(0, 2, False)
-        quantize_w1(0, 0, 2)
+        quantize_w1(0, 2)
         for t in range(2):
             first_layer(0, t, 0)
         round_w1(1, 0, True)
         round_w1(1, 2, False)
-        quantize_w1(0, 2, 4)
-        for t in range(2, PACK):
-            first_layer(0, t, 0)
-        for t in range(PACK):
-            quantize_w1(1, t, t + 1)
-            first_layer(1, t, 0)
+        quantize_w1(2, 3)
+        first_layer(1, 0, 0)
+        quantize_w1(3, 5)
+        first_layer(1, 1, 0)
+        first_layer(0, 2, 0)
+        quantize_w1(5, 7)
+        first_layer(1, 2, 0)
+        first_layer(0, 3, 0)
+        quantize_w1(7, 8)
+        first_layer(1, 3, 0)
         picked_planes.append(keep.tile([P, HALF], U8, name="picked_planes1", tag="raw1", align_bytes=64))
         pick(picked_planes[1], planes, HALF, S)
         for t in range(PACK):
             first_layer(1, t, 1)
             first_layer(0, t, 1)
-
-        w2_bf = keep.tile([P, N * PACK], BF16, name="w2_bf", align_bytes=64)
-        w2_codes = keep.tile([P, N], U32, name="w2_codes", align_bytes=64)
-        w2_scales = keep.tile([P, N], U8, name="w2_scales", align_bytes=64)
-        nc.scalar.copy(
-            out=w2_bf[:].rearrange("p (c i j) -> p c j i", i=4, j=PACK),
-            in_=w2_raw[:].rearrange("p j (c i) -> p c j i", i=4),
-        )
 
         z = [keep.tile([P, PACK, HALF], BF16, name=f"z{hf}", align_bytes=64) for hf in range(2)]
 
@@ -234,14 +232,22 @@ def tile_picked_dconv_none_e_kernel(tc, xT, w1, w2, taps, offs, out):
         for hf in range(2):
             for t in range(PACK):
                 late_term(t, hf)
+        w2_bf = keep.tile([P, N * PACK], BF16, name="w2_bf", tag="planes", align_bytes=64)
+        w2_codes = keep.tile([P, N], U32, name="w2_codes", align_bytes=64)
+        w2_scales = keep.tile([P, N], U8, name="w2_scales", align_bytes=64)
+        nc.scalar.copy(
+            out=w2_bf[:].rearrange("p (c i j) -> p c j i", i=4, j=PACK),
+            in_=w2_raw[:].rearrange("p j (c i) -> p c j i", i=4),
+        )
+
         first_sum(0, 0)
-        nc.vector.quantize_mx(out=w2_codes[:].bitcast(FP8X4), scales=w2_scales[:], in_=w2_bf[:])
         for t in range(1, PACK):
             first_sum(t, 0)
             second_sum(t - 1, 0, HALF)
         first_sum(0, 1)
         second_sum(PACK - 1, 0, HALF)
         weave(0)
+        nc.vector.quantize_mx(out=w2_codes[:].bitcast(FP8X4), scales=w2_scales[:], in_=w2_bf[:])
         for t in range(1, PACK):
             first_sum(t, 1)
             second_sum(t - 1, *RANGES[1])

from contextlib import ExitStack

import concourse.mybir as mybir

K, T, S, D, H, N = 1024, 1024, 512, 3, 512, 128
FLOPS = 2 * K * H * S + 2 * H * N * S

F32 = mybir.dt.float32
BF16 = mybir.dt.bfloat16
U32 = mybir.dt.uint32
I32 = mybir.dt.int32
U16 = mybir.dt.uint16
U8 = mybir.dt.uint8
FP8X4 = mybir.dt.float8_e4m3fn_x4
MULT = mybir.AluOpType.mult
ADD = mybir.AluOpType.add
COPY = mybir.ActivationFunctionType.Copy

P = 128
PACK = 4
K_PASS = P * PACK
PASSES = K // K_PASS
PAD = 8
HALF = S // 2
X_CHUNKS = ((0, 0, 1024), (1, 0, 512), (1, 512, 1024))
PLANE_STEP = 4
W1_SLOTS = ((0, 0), (0, 1), (1, 0), (1, 1), (0, 2), (0, 3), (1, 2), (1, 3))
RANGES = ((0, 256), (256, 384), (384, 512))


def tile_picked_dconv_none_e_kernel(tc, xT, w1, w2, taps, offs, out):
    nc = tc.nc
    with ExitStack() as ctx:
        keep = ctx.enter_context(tc.tile_pool(name="keep", bufs=1))
        psum = ctx.enter_context(tc.psum_pool(name="psum", bufs=1))

        offsets = keep.tile([P, S // 16], U16, name="offsets")
        tap = keep.tile([P, PACK * D], F32, name="tap")
        x_raw = [keep.tile([P, PACK, b - a], F32, name=f"x_raw{i}") for i, (g, a, b) in enumerate(X_CHUNKS)]
        w1_raw = [keep.tile([P, PACK, H], F32, name=f"w1_raw{g}", tag=f"raw{g}", align_bytes=64) for g in range(PASSES)]
        w2_raw = keep.tile([P, PACK, N], F32, name="w2_raw")

        x_rows = xT.rearrange("(g p j) t -> g p j t", g=PASSES, j=PACK)
        w1_rows = w1.rearrange("(g p j) h -> g p j h", g=PASSES, j=PACK)
        for i, (g, a, b) in enumerate(X_CHUNKS):
            nc.sync.dma_start(out=x_raw[i][:], in_=x_rows[g, :, :, a:b])
            if i == 0:
                nc.sync.dma_start(offsets[:], offs)
        for g in range(PASSES):
            nc.sync.dma_start(out=w1_raw[g][:], in_=w1_rows[g])
        nc.sync.dma_start(out=tap[:], in_=taps.rearrange("(p t) d -> p (t d)", t=PACK))
        nc.sync.dma_start(out=w2_raw[:], in_=w2.rearrange("(p j) n -> p j n", j=PACK))

        late = keep.tile([P, PACK, PAD + S], F32, name="late")
        mid = keep.tile([P, PACK, 2 * PAD + S], F32, name="mid")
        planes = keep.tile([P, T], U8, name="planes", tag="planes", align_bytes=64)
        nc.vector.memset(planes[:].bitcast(I32), 0)
        nc.vector.memset(mid[:, :, 0 : PAD + 1], 0.0)
        nc.scalar.activation(out=late[:, :, 0:PAD], in_=mid[:, :, 0:PAD], func=COPY)

        x_bf = [keep.tile([P, T * PACK], BF16, name=f"x_bf{g}", align_bytes=64) for g in range(PASSES)]
        words = [keep.tile([P, T], U32, name=f"words{g}", align_bytes=64) for g in range(PASSES)]
        picked = [keep.tile([P, S], U32, name=f"picked{g}", align_bytes=64) for g in range(PASSES)]
        picked_planes = [keep.tile([P, HALF], U8, name="picked_planes0", align_bytes=64)]

        def round_x(i, a, b, on_vector):
            g, first, last = X_CHUNKS[i]
            dst = x_bf[g][:, a * PACK : b * PACK].rearrange("p (c i j) -> p c j i", i=4, j=PACK)
            src = x_raw[i][:, :, a - first : b - first].rearrange("p j (c i) -> p c j i", i=4)
            if on_vector:
                nc.vector.tensor_copy(out=dst, in_=src)
            else:
                nc.scalar.activation(out=dst, in_=src, func=COPY)

        def quantize_x(g, a, b):
            nc.vector.quantize_mx(
                out=words[g][:, a:b].bitcast(FP8X4),
                scales=planes[PLANE_STEP * g :, a:b],
                in_=x_bf[g][:, a * PACK : b * PACK],
            )

        def pick(dst, window, a, b):
            nc.vector.tensor_copy(out=dst[:], in_=window[:].indirect(offsets[:, a // 16 : b // 16]))

        w1_bf = keep.tile([P, len(W1_SLOTS), P, PACK], BF16, name="w1_bf", align_bytes=64)
        w1_q = {}

        def round_w1(g, ta, on_vector):
            first = W1_SLOTS.index((g, ta))
            dst = w1_bf[:, first : first + 2].rearrange("p t m j -> p m j t")
            src = w1_raw[g][:].rearrange("p j (m t) -> p m j t", t=PACK)[:, :, :, ta : ta + 2]
            if on_vector:
                nc.vector.tensor_copy(out=dst, in_=src)
            else:
                nc.scalar.copy(out=dst, in_=src)

        def quantize_w1(first, last):
            codes = keep.tile([P, (last - first) * P], U32, name=f"w1_codes{first}", align_bytes=64)
            scales = keep.tile([P, (last - first) * P], U8, name=f"w1_scales{first}", align_bytes=64)
            nc.vector.quantize_mx(
                out=codes[:].bitcast(FP8X4),
                scales=scales[:],
                in_=w1_bf[:, first:last].rearrange("p t m j -> p (t m j)"),
            )
            for slot in range(first, last):
                cols = slice((slot - first) * P, (slot - first + 1) * P)
                w1_q[W1_SLOTS[slot]] = (codes[:, cols], scales[:, cols])

        h = [[psum.tile([P, HALF], F32, name=f"h{t}{hf}", tag=f"bank{t}{hf}") for hf in range(2)] for t in range(PACK)]

        def first_layer(g, t, hf):
            nc.tensor.matmul_mx(
                out=h[t][hf][:],
                lhsT=w1_q[g, t][0].bitcast(FP8X4),
                lhsT_scale=w1_q[g, t][1],
                rhs=picked[g][:, hf * HALF : (hf + 1) * HALF].bitcast(FP8X4),
                rhs_scale=picked_planes[hf][PLANE_STEP * g :, :],
                start=(g == hf),
                stop=(g != hf),
            )

        round_x(0, 640, 1024, False)
        round_x(0, 0, 512, True)
        round_x(0, 512, 640, True)
        quantize_x(0, 0, 512)
        quantize_x(0, 512, 1024)
        pick(picked[0], words[0], 0, S)
        round_x(1, 0, 256, False)
        round_x(1, 256, 512, False)
        quantize_x(1, 0, 256)
        round_x(2, 832, 1024, False)
        round_x(2, 512, 768, True)
        round_x(2, 768, 832, True)
        quantize_x(1, 256, 768)
        quantize_x(1, 768, 1024)
        pick(picked_planes[0], planes, 0, HALF)
        pick(picked[1], words[1], 0, S)
        round_w1(0, 0, False)
        round_w1(0, 2, False)
        quantize_w1(0, 2)
        for t in range(2):
            first_layer(0, t, 0)
        round_w1(1, 0, True)
        round_w1(1, 2, False)
        quantize_w1(2, 3)
        first_layer(1, 0, 0)
        quantize_w1(3, 5)
        first_layer(1, 1, 0)
        first_layer(0, 2, 0)
        quantize_w1(5, 7)
        first_layer(1, 2, 0)
        first_layer(0, 3, 0)
        quantize_w1(7, 8)
        first_layer(1, 3, 0)
        picked_planes.append(keep.tile([P, HALF], U8, name="picked_planes1", tag="raw1", align_bytes=64))
        pick(picked_planes[1], planes, HALF, S)
        for t in range(PACK):
            first_layer(1, t, 1)
            first_layer(0, t, 1)

        z = [keep.tile([P, PACK, HALF], BF16, name=f"z{hf}", align_bytes=64) for hf in range(2)]

        def late_term(t, hf):
            a = PAD + hf * HALF
            nc.scalar.activation(out=late[:, t, a : a + HALF], in_=h[t][hf][:], func=COPY, scale=tap[:, D * t + 2 : D * t + 3])

        def first_sum(t, hf):
            a = PAD + hf * HALF
            nc.vector.scalar_tensor_tensor(
                out=mid[:, t, a + 1 : a + HALF + 1],
                in0=h[t][hf][:],
                scalar=tap[:, D * t + 1 : D * t + 2],
                in1=late[:, t, a - 1 : a + HALF - 1],
                op0=MULT,
                op1=ADD,
            )

        def second_sum(t, a, b):
            hf, a0 = divmod(a, HALF)
            nc.vector.scalar_tensor_tensor(
                out=z[hf][:, t, a0 : a0 + b - a],
                in0=h[t][hf][:, a0 : a0 + b - a],
                scalar=tap[:, D * t : D * t + 1],
                in1=mid[:, t, PAD + a : PAD + b],
                op0=MULT,
                op1=ADD,
            )

        woven = [keep.tile([P, (b - a) * PACK], BF16, name=f"woven{r}", align_bytes=64) for r, (a, b) in enumerate(RANGES)]

        def weave(r):
            a, b = RANGES[r]
            hf, a0 = divmod(a, HALF)
            dst = woven[r][:].rearrange("p (c i t) -> p c t i", i=4, t=PACK)
            src = z[hf][:, :, a0 : a0 + b - a].rearrange("p t (c i) -> p c t i", i=4)
            nc.scalar.copy(out=dst, in_=src)

        last_a, last_b = RANGES[-1]
        early = keep.tile([P, PACK, last_b - last_a], F32, name="early")

        def early_term(t):
            nc.scalar.activation(out=early[:, t, :], in_=h[t][1][:, last_a - HALF :], func=COPY, scale=tap[:, D * t : D * t + 1])

        def woven_sum():
            nc.vector.tensor_tensor(
                out=woven[-1][:].rearrange("p (c i t) -> p c t i", i=4, t=PACK),
                in0=early[:].rearrange("p t (c i) -> p c t i", i=4),
                in1=mid[:, :, PAD + last_a : PAD + last_b].rearrange("p t (c i) -> p c t i", i=4),
                op=ADD,
            )

        def second_layer(r):
            a, b = RANGES[r]
            codes = keep.tile([P, b - a], U32, name=f"z_codes{r}", align_bytes=64)
            scales = keep.tile([P, b - a], U8, name=f"z_scales{r}", align_bytes=64)
            nc.vector.quantize_mx(out=codes[:].bitcast(FP8X4), scales=scales[:], in_=woven[r][:])
            acc = psum.tile([P, HALF], F32, name=f"acc{r}", tag=f"bank{r}0")
            nc.tensor.matmul_mx(
                out=acc[:, : b - a],
                lhsT=w2_codes[:].bitcast(FP8X4),
                lhsT_scale=w2_scales[:],
                rhs=codes[:].bitcast(FP8X4),
                rhs_scale=scales[:],
                start=True,
                stop=True,
            )
            result = keep.tile([P, b - a], F32, name=f"result{r}")
            nc.scalar.copy(out=result[:], in_=acc[:, : b - a])
            queue = nc.scalar if r == len(RANGES) - 1 else nc.sync
            queue.dma_start(out=out[:, a:b], in_=result[:])

        for hf in range(2):
            for t in range(PACK):
                late_term(t, hf)
        w2_bf = keep.tile([P, N * PACK], BF16, name="w2_bf", tag="planes", align_bytes=64)
        w2_codes = keep.tile([P, N], U32, name="w2_codes", align_bytes=64)
        w2_scales = keep.tile([P, N], U8, name="w2_scales", align_bytes=64)
        nc.scalar.copy(
            out=w2_bf[:].rearrange("p (c i j) -> p c j i", i=4, j=PACK),
            in_=w2_raw[:].rearrange("p j (c i) -> p c j i", i=4),
        )

        first_sum(0, 0)
        for t in range(1, PACK):
            first_sum(t, 0)
            second_sum(t - 1, 0, HALF)
        first_sum(0, 1)
        second_sum(PACK - 1, 0, HALF)
        weave(0)
        nc.vector.quantize_mx(out=w2_codes[:].bitcast(FP8X4), scales=w2_scales[:], in_=w2_bf[:])
        for t in range(1, PACK):
            first_sum(t, 1)
            second_sum(t - 1, *RANGES[1])
        second_sum(PACK - 1, *RANGES[1])
        for t in range(PACK):
            early_term(t)
        weave(1)
        second_layer(0)
        woven_sum()
        second_layer(1)
        second_layer(2)
